import numpy as np
import ml_dtypes

BF16 = ml_dtypes.bfloat16


def bf(x):
    return np.asarray(x, np.float32).astype(BF16)


def f32(x):
    return np.asarray(x, np.float32)


def f64(x):
    return np.asarray(x).astype(np.float64)


def striped(idx):
    return np.tile(idx.reshape(-1, 16).T, (8, 1))


def rows(idx, k):
    return np.tile(idx, (k, 1))


def look(tab, idx):
    return np.take_along_axis(f64(tab), rows(idx, len(tab)), axis=1)


K, S, V, N, M = 256, 256, 256, 256, 512


def setup_inputs():
    return {"tab": f32(np.random.standard_normal((K, S))), "y": f32(np.random.standard_normal((K, V))), "w": bf(np.random.standard_normal((K, M)) / np.sqrt(K)), "b": f32(0.5 * np.random.standard_normal((M, 1))), "offs": striped(np.random.permutation(S)[:N])}


def reference(tab, y, w, b, offs):
    idx = offs[:16].T.reshape(-1)
    t = look(tab, idx)
    x = np.tanh(t) * f64(y)
    y = f64(w).T @ x
    return np.maximum(y + f64(b), 0.0)

@@ -1,0 +1,73 @@
+import concourse.mybir as mybir
+
+F32, BF16, U16 = mybir.dt.float32, mybir.dt.bfloat16, mybir.dt.uint16
+ADD, MAX, MULT = mybir.AluOpType.add, mybir.AluOpType.max, mybir.AluOpType.mult
+TANH, RELU = mybir.ActivationFunctionType.Tanh, mybir.ActivationFunctionType.Relu
+
+P = 128
+ROWS, COLS = 256, 256
+N, M = 256, 512
+K_BLOCKS = ROWS // P
+M_BLOCKS = M // P
+PIECE = 128
+STRIPE = 16
+
+FLOPS = 2 * ROWS * M * N
+
+
+def tile_lookup_gate_tanh_relu_kernel(tc, tab, y, w, b, offs, out):
+    nc = tc.nc
+    tab_rows = tab.rearrange("(p k) s -> p k s", k=K_BLOCKS)
+    y_rows = y.rearrange("(p k) j -> p k j", k=K_BLOCKS)
+    w_rows = w.rearrange("(p k) m -> p k m", k=K_BLOCKS)
+    b_rows = b.rearrange("(p q) o -> p (q o)", q=M_BLOCKS)
+    out_rows = out.rearrange("(p q) j -> p q j", q=M_BLOCKS)
+
+    with (
+        tc.tile_pool(name="held", bufs=1) as held,
+        tc.tile_pool(name="work", bufs=4) as work,
+        tc.psum_pool(name="psum", bufs=8) as psum,
+    ):
+        offsets = held.tile([P, N // STRIPE], U16, name="offsets")
+        nc.sync.dma_start(offsets[:], offs)
+        tables = []
+        for k in range(K_BLOCKS):
+            table = held.tile([P, COLS], F32, name=f"table{k}")
+            nc.sync.dma_start(table[:], tab_rows[:, k, :])
+            tables.append(table)
+        stream = held.tile([P, K_BLOCKS, N], F32, name="stream")
+        nc.sync.dma_start(stream[:], y_rows)
+        weights = held.tile([P, K_BLOCKS, M], BF16, name="weights")
+        nc.scalar.dma_start(weights[:], w_rows)
+        bias = held.tile([P, M_BLOCKS], F32, name="bias")
+        nc.scalar.dma_start(bias[:], b_rows)
+
+        for piece in range(N // PIECE):
+            columns = slice(piece * PIECE, (piece + 1) * PIECE)
+            entries = offsets[:, piece * PIECE // STRIPE : (piece + 1) * PIECE // STRIPE]
+            gated = []
+            for k in range(K_BLOCKS):
+                gate = work.tile([P, PIECE], F32, name="gate")
+                nc.scalar.activation(gate[:], tables[k][:].indirect(entries), TANH)
+                x = work.tile([P, PIECE], BF16, name="x")
+                nc.vector.tensor_tensor(x[:], gate[:], stream[:, k, columns], MULT)
+                gated.append(x)
+
+            sums = [psum.tile([P, PIECE], F32, name="sum") for q in range(M_BLOCKS)]
+            for k in range(K_BLOCKS):
+                for q in range(M_BLOCKS):
+                    nc.tensor.matmul(
+                        sums[q][:],
+                        weights[:, k, q::M_BLOCKS],
+                        gated[k][:],
+                        start=k == 0,
+                        stop=k == K_BLOCKS - 1,
+                    )
+
+            result = work.tile([P, M_BLOCKS, PIECE], F32, name="result")
+            for q in range(M_BLOCKS):
+                if q % 2 == 0:
+                    nc.vector.tensor_scalar(result[:, q, :], sums[q][:], bias[:, q : q + 1], 0.0, ADD, MAX)
+                else:
+                    nc.scalar.activation(result[:, q, :], sums[q][:], RELU, bias=bias[:, q : q + 1])
+            nc.sync.dma_start(out_rows[:, :, columns], result[:])

@@ -28,6 +28,11 @@ def tile_lookup_gate_tanh_relu_kernel(tc, tab, y, w, b, offs, out):
         tc.tile_pool(name="work", bufs=4) as work,
         tc.psum_pool(name="psum", bufs=8) as psum,
     ):
+        zero = held.tile([P, 1], F32, name="zero")
+        nc.vector.memset(zero[:], 0.0)
+        warm = held.tile([P, 1], F32, name="warm")
+        nc.scalar.activation(warm[:], zero[:], TANH)
+
         offsets = held.tile([P, N // STRIPE], U16, name="offsets")
         nc.sync.dma_start(offsets[:], offs)
         tables = []
@@ -38,9 +43,9 @@ def tile_lookup_gate_tanh_relu_kernel(tc, tab, y, w, b, offs, out):
         stream = held.tile([P, K_BLOCKS, N], F32, name="stream")
         nc.sync.dma_start(stream[:], y_rows)
         weights = held.tile([P, K_BLOCKS, M], BF16, name="weights")
-        nc.scalar.dma_start(weights[:], w_rows)
+        nc.gpsimd.dma_start(weights[:], w_rows)
         bias = held.tile([P, M_BLOCKS], F32, name="bias")
-        nc.scalar.dma_start(bias[:], b_rows)
+        nc.gpsimd.dma_start(bias[:], b_rows)
 
         for piece in range(N // PIECE):
             columns = slice(piece * PIECE, (piece + 1) * PIECE)

@@ -11,6 +11,8 @@ K_BLOCKS = ROWS // P
 M_BLOCKS = M // P
 PIECE = 128
 STRIPE = 16
+WARM_COLS = 512
+WARM_PRODUCTS = 6
 
 FLOPS = 2 * ROWS * M * N
 
@@ -32,6 +34,12 @@ def tile_lookup_gate_tanh_relu_kernel(tc, tab, y, w, b, offs, out):
         nc.vector.memset(zero[:], 0.0)
         warm = held.tile([P, 1], F32, name="warm")
         nc.scalar.activation(warm[:], zero[:], TANH)
+
+        blank = held.tile([P, WARM_COLS], BF16, name="blank")
+        nc.vector.memset(blank[:], 0.0)
+        idle = psum.tile([P, WARM_COLS], F32, name="idle", tag="sum")
+        for step in range(WARM_PRODUCTS):
+            nc.tensor.matmul(idle[:], blank[:, :P], blank[:], start=True, stop=True)
 
         offsets = held.tile([P, N // STRIPE], U16, name="offsets")
         nc.sync.dma_start(offsets[:], offs)
@@ -58,7 +66,7 @@ def tile_lookup_gate_tanh_relu_kernel(tc, tab, y, w, b, offs, out):
                 nc.vector.tensor_tensor(x[:], gate[:], stream[:, k, columns], MULT)
                 gated.append(x)
 
-            sums = [psum.tile([P, PIECE], F32, name="sum") for q in range(M_BLOCKS)]
+            sums = [psum.tile([P, PIECE], F32, name="sum", tag="sum") for q in range(M_BLOCKS)]
             for k in range(K_BLOCKS):
                 for q in range(M_BLOCKS):
                     nc.tensor.matmul(
@@ -75,4 +83,5 @@ def tile_lookup_gate_tanh_relu_kernel(tc, tab, y, w, b, offs, out):
                     nc.vector.tensor_scalar(result[:, q, :], sums[q][:], bias[:, q : q + 1], 0.0, ADD, MAX)
                 else:
                     nc.scalar.activation(result[:, q, :], sums[q][:], RELU, bias=bias[:, q : q + 1])
-            nc.sync.dma_start(out_rows[:, :, columns], result[:])
+                if q % 2 == 1:
+                    nc.sync.dma_start(out_rows[:, q - 1 : q + 1, columns], result[:, q - 1 : q + 1, :])

@@ -12,7 +12,7 @@ M_BLOCKS = M // P
 PIECE = 128
 STRIPE = 16
 WARM_COLS = 512
-WARM_PRODUCTS = 6
+WARM_PRODUCTS = 4
 
 FLOPS = 2 * ROWS * M * N
 
@@ -30,6 +30,20 @@ def tile_lookup_gate_tanh_relu_kernel(tc, tab, y, w, b, offs, out):
         tc.tile_pool(name="work", bufs=4) as work,
         tc.psum_pool(name="psum", bufs=8) as psum,
     ):
+        offsets = held.tile([P, N // STRIPE], U16, name="offsets")
+        nc.sync.dma_start(offsets[:], offs)
+        table0 = held.tile([P, COLS], F32, name="table0")
+        nc.scalar.dma_start(table0[:], tab_rows[:, 0, :])
+        table1 = held.tile([P, COLS], F32, name="table1")
+        nc.sync.dma_start(table1[:], tab_rows[:, 1, :])
+        tables = [table0, table1]
+        stream = held.tile([P, K_BLOCKS, N], F32, name="stream")
+        nc.scalar.dma_start(stream[:], y_rows)
+        weights = held.tile([P, K_BLOCKS, M], BF16, name="weights")
+        nc.sync.dma_start(weights[:], w_rows)
+        bias = held.tile([P, M_BLOCKS], F32, name="bias")
+        nc.sync.dma_start(bias[:], b_rows)
+
         zero = held.tile([P, 1], F32, name="zero")
         nc.vector.memset(zero[:], 0.0)
         warm = held.tile([P, 1], F32, name="warm")
@@ -40,20 +54,6 @@ def tile_lookup_gate_tanh_relu_kernel(tc, tab, y, w, b, offs, out):
         idle = psum.tile([P, WARM_COLS], F32, name="idle", tag="sum")
         for step in range(WARM_PRODUCTS):
             nc.tensor.matmul(idle[:], blank[:, :P], blank[:], start=True, stop=True)
-
-        offsets = held.tile([P, N // STRIPE], U16, name="offsets")
-        nc.sync.dma_start(offsets[:], offs)
-        tables = []
-        for k in range(K_BLOCKS):
-            table = held.tile([P, COLS], F32, name=f"table{k}")
-            nc.sync.dma_start(table[:], tab_rows[:, k, :])
-            tables.append(table)
-        stream = held.tile([P, K_BLOCKS, N], F32, name="stream")
-        nc.sync.dma_start(stream[:], y_rows)
-        weights = held.tile([P, K_BLOCKS, M], BF16, name="weights")
-        nc.gpsimd.dma_start(weights[:], w_rows)
-        bias = held.tile([P, M_BLOCKS], F32, name="bias")
-        nc.gpsimd.dma_start(bias[:], b_rows)
 
         for piece in range(N // PIECE):
             columns = slice(piece * PIECE, (piece + 1) * PIECE)

import concourse.mybir as mybir

F32, BF16, U16 = mybir.dt.float32, mybir.dt.bfloat16, mybir.dt.uint16
ADD, MAX, MULT = mybir.AluOpType.add, mybir.AluOpType.max, mybir.AluOpType.mult
TANH, RELU = mybir.ActivationFunctionType.Tanh, mybir.ActivationFunctionType.Relu

P = 128
ROWS, COLS = 256, 256
N, M = 256, 512
K_BLOCKS = ROWS // P
M_BLOCKS = M // P
PIECE = 128
STRIPE = 16
WARM_COLS = 512
WARM_PRODUCTS = 4

FLOPS = 2 * ROWS * M * N


def tile_lookup_gate_tanh_relu_kernel(tc, tab, y, w, b, offs, out):
    nc = tc.nc
    tab_rows = tab.rearrange("(p k) s -> p k s", k=K_BLOCKS)
    y_rows = y.rearrange("(p k) j -> p k j", k=K_BLOCKS)
    w_rows = w.rearrange("(p k) m -> p k m", k=K_BLOCKS)
    b_rows = b.rearrange("(p q) o -> p (q o)", q=M_BLOCKS)
    out_rows = out.rearrange("(p q) j -> p q j", q=M_BLOCKS)

    with (
        tc.tile_pool(name="held", bufs=1) as held,
        tc.tile_pool(name="work", bufs=4) as work,
        tc.psum_pool(name="psum", bufs=8) as psum,
    ):
        offsets = held.tile([P, N // STRIPE], U16, name="offsets")
        nc.sync.dma_start(offsets[:], offs)
        table0 = held.tile([P, COLS], F32, name="table0")
        nc.scalar.dma_start(table0[:], tab_rows[:, 0, :])
        table1 = held.tile([P, COLS], F32, name="table1")
        nc.sync.dma_start(table1[:], tab_rows[:, 1, :])
        tables = [table0, table1]
        stream = held.tile([P, K_BLOCKS, N], F32, name="stream")
        nc.scalar.dma_start(stream[:], y_rows)
        weights = held.tile([P, K_BLOCKS, M], BF16, name="weights")
        nc.sync.dma_start(weights[:], w_rows)
        bias = held.tile([P, M_BLOCKS], F32, name="bias")
        nc.sync.dma_start(bias[:], b_rows)

        zero = held.tile([P, 1], F32, name="zero")
        nc.vector.memset(zero[:], 0.0)
        warm = held.tile([P, 1], F32, name="warm")
        nc.scalar.activation(warm[:], zero[:], TANH)

        blank = held.tile([P, WARM_COLS], BF16, name="blank")
        nc.vector.memset(blank[:], 0.0)
        idle = psum.tile([P, WARM_COLS], F32, name="idle", tag="sum")
        for step in range(WARM_PRODUCTS):
            nc.tensor.matmul(idle[:], blank[:, :P], blank[:], start=True, stop=True)

        for piece in range(N // PIECE):
            columns = slice(piece * PIECE, (piece + 1) * PIECE)
            entries = offsets[:, piece * PIECE // STRIPE : (piece + 1) * PIECE // STRIPE]
            gated = []
            for k in range(K_BLOCKS):
                gate = work.tile([P, PIECE], F32, name="gate")
                nc.scalar.activation(gate[:], tables[k][:].indirect(entries), TANH)
                x = work.tile([P, PIECE], BF16, name="x")
                nc.vector.tensor_tensor(x[:], gate[:], stream[:, k, columns], MULT)
                gated.append(x)

            sums = [psum.tile([P, PIECE], F32, name="sum", tag="sum") for q in range(M_BLOCKS)]
            for k in range(K_BLOCKS):
                for q in range(M_BLOCKS):
                    nc.tensor.matmul(
                        sums[q][:],
                        weights[:, k, q::M_BLOCKS],
                        gated[k][:],
                        start=k == 0,
                        stop=k == K_BLOCKS - 1,
                    )

            result = work.tile([P, M_BLOCKS, PIECE], F32, name="result")
            for q in range(M_BLOCKS):
                if q % 2 == 0:
                    nc.vector.tensor_scalar(result[:, q, :], sums[q][:], bias[:, q : q + 1], 0.0, ADD, MAX)
                else:
                    nc.scalar.activation(result[:, q, :], sums[q][:], RELU, bias=bias[:, q : q + 1])
                if q % 2 == 1:
                    nc.sync.dma_start(out_rows[:, q - 1 : q + 1, columns], result[:, q - 1 : q + 1, :])
